import numpy as np
import ml_dtypes


def mxq(x, axis, fmt="e4m3"):
    dtype, down = {"e4m3": (ml_dtypes.float8_e4m3fn, 7), "e5m2": (ml_dtypes.float8_e5m2, 14)}[fmt]
    v = np.moveaxis(np.asarray(x, np.float32).astype(ml_dtypes.bfloat16).astype(np.float64), axis, -1)
    blocks = v.reshape(v.shape[:-1] + (-1, 32))
    amax = np.abs(blocks).max(-1, keepdims=True)
    byte = np.maximum(np.where(amax > 0, np.frexp(amax)[1] - 1 + 127, 0) - down, 1)
    scale = np.exp2(byte - 127.0)
    codes = (blocks / scale).astype(np.float32).astype(dtype).astype(np.float64)
    return np.moveaxis((codes * scale).reshape(v.shape), -1, axis)


WIDE = False


def mx_kscale(k):
    if not WIDE:
        return np.ones(k)
    levels = np.array([10, -10, 5, -5, 0])
    if k % 512:
        return np.exp2(np.random.permutation(np.resize(levels, k // 32))).repeat(32)
    a = np.empty((k // 512, 16))
    for p in range(k // 512):
        a[p, :8] = np.random.permutation(np.resize(levels, 8))
        for g in range(8):
            far = levels[np.abs(levels - a[p, g]) >= 10]
            a[p, g + 8] = far[np.random.randint(len(far))]
    return np.exp2(a.ravel()).repeat(32)


def f64(x):
    return np.asarray(x).astype(np.float64)


def striped8(idx):
    return np.asarray(idx).reshape(8, -1, 16).transpose(0, 2, 1).reshape(128, -1).astype(np.uint16)


def unstriped8(offs):
    return offs.reshape(8, 16, -1).transpose(0, 2, 1).reshape(8, -1).astype(np.int64)


def pick8(x, idx, run):
    r = np.arange(len(x))
    return x[r[:, None], idx[r % (8 * run) // run]]


E2M1 = np.array([0.0, 0.5, 1.0, 1.5, 2.0, 3.0, 4.0, 6.0, -0.0, -0.5, -1.0, -1.5, -2.0, -3.0, -4.0, -6.0])


def pack_weight(w, fmt):
    k, n = w.shape
    w = f64(np.asarray(w, np.float32).astype(ml_dtypes.bfloat16)).reshape(k // 32, 32, n)
    amax = np.abs(w).max(1)
    if fmt == "e4m3":
        byte = np.frexp(amax)[1] - 1 + 127 - 7
    else:
        mant, ex = np.frexp(amax / 6.0)
        byte = np.where(mant > 0.5, ex, ex - 1) + 127
    byte = np.clip(np.where(amax > 0, byte, 1), 1, 254)
    scaled = (w * np.exp2(127.0 - byte)[:, None, :]).reshape(k, n).astype(np.float32)
    by_word = np.ascontiguousarray(scaled.reshape(k // 512, 128, 4, n).transpose(0, 1, 3, 2))
    if fmt == "e4m3":
        words = by_word.astype(ml_dtypes.float8_e4m3fn).view(np.uint8)
    else:
        c = by_word.astype(ml_dtypes.float4_e2m1fn).view(np.uint8) & 0xF
        words = (c[..., 0::2] | (c[..., 1::2] << 4)).reshape(k // 512, 128, 2 * n)
    return np.ascontiguousarray(words), np.ascontiguousarray(byte.astype(np.uint8).reshape(k // 512, 16, n))


def unpack_weight(words, scales, fmt):
    g, _, n = scales.shape
    words = np.ascontiguousarray(words).reshape(g, 128, n, -1)
    if fmt == "e4m3":
        vals = words.view(ml_dtypes.float8_e4m3fn).astype(np.float64)
    else:
        nib = np.empty((g, 128, n, 4), np.uint8)
        nib[..., 0::2] = words & 0xF
        nib[..., 1::2] = words >> 4
        vals = E2M1[nib]
    vals = vals * np.repeat(np.exp2(scales.astype(np.float64) - 127.0), 8, axis=1)[..., None]
    return vals.transpose(0, 1, 3, 2).reshape(g * 512, n)


D, K, T, U, X, S, I, Q = 512, 512, 1024, 1024, 1024, 1024, 512, 128


def setup_inputs():
    n = np.random.standard_normal
    idx = np.stack([np.random.permutation(T)[:I] for _ in range(8)])
    idx2 = np.stack([np.random.permutation(U)[:I] for _ in range(8)])
    idx3 = np.stack([np.random.permutation(X)[:I] for _ in range(8)])
    idx4 = np.stack([np.random.permutation(S)[:I] for _ in range(8)])
    idx5 = np.stack([np.random.permutation(S)[:I] for _ in range(8)])
    idx6 = np.stack([np.random.permutation(T)[:I] for _ in range(8)])
    fd = mx_kscale(D)
    fk = mx_kscale(K)
    wqp = pack_weight(n((D, K)) * 1.0 / np.sqrt(D) * fd[:, None] * fk, "e4m3")
    keysp = pack_weight(n((K, T)) * 1.0 / np.sqrt(K) / fk[:, None], "e4m3")
    notesp = pack_weight(n((K, U)) * 1.0 / np.sqrt(K) / fk[:, None], "e2m1")
    usersp = pack_weight(n((D, X)) * 1.0 / np.sqrt(D) * fd[:, None], "e4m3")
    shelvesp = pack_weight(n((D, S)) * 1.0 / np.sqrt(D) * fd[:, None], "e2m1")
    return {
        "states": (n((D, Q)) * 0.95 / fd[:, None]).astype(np.float32),
        "wq_words": wqp[0],
        "wq_scales": wqp[1],
        "keys_words": keysp[0],
        "keys_scales": keysp[1],
        "notes_words": notesp[0],
        "notes_scales": notesp[1],
        "users_words": usersp[0],
        "users_scales": usersp[1],
        "shelves_words": shelvesp[0],
        "shelves_scales": shelvesp[1],
        "offs": striped8(idx),
        "offs2": striped8(idx2),
        "offs3": striped8(idx3),
        "offs4": striped8(idx4),
        "offs5": striped8(idx5),
        "offs6": striped8(idx6),
    }


def reference(states, wq_words, wq_scales, keys_words, keys_scales, notes_words, notes_scales, users_words, users_scales, shelves_words, shelves_scales, offs, offs2, offs3, offs4, offs5, offs6):
    idx = unstriped8(offs)
    idx2 = unstriped8(offs2)
    idx3 = unstriped8(offs3)
    idx4 = unstriped8(offs4)
    idx5 = unstriped8(offs5)
    idx6 = unstriped8(offs6)
    wqu = unpack_weight(wq_words, wq_scales, "e4m3")
    keysu = unpack_weight(keys_words, keys_scales, "e4m3")
    notesu = unpack_weight(notes_words, notes_scales, "e2m1")
    usersu = unpack_weight(users_words, users_scales, "e4m3")
    shelvesu = unpack_weight(shelves_words, shelves_scales, "e2m1")
    statesq = mxq(f64(states), 0, "e4m3")
    qv = wqu.T @ statesq
    qvq = mxq(qv, 0, "e4m3")
    a = qvq.T @ keysu
    b = qvq.T @ notesu
    c0 = statesq.T @ usersu
    d0 = statesq.T @ shelvesu
    hi1 = np.maximum(pick8(a, idx, 16), pick8(b, idx2, 16))
    lo1 = np.minimum(pick8(a, idx, 16), pick8(b, idx2, 16))
    hi2 = np.maximum(pick8(c0, idx3, 16), pick8(d0, idx4, 16))
    lo2 = np.minimum(pick8(c0, idx3, 16), pick8(d0, idx4, 16))
    m1 = np.minimum(hi1, hi2)
    m2 = np.maximum(lo1, lo2)
    f1 = np.zeros((Q, S))
    f1[np.arange(Q)[:, None], idx4[np.arange(Q) % 128 // 16]] = m1
    f2 = np.zeros((Q, T))
    f2[np.arange(Q)[:, None], idx[np.arange(Q) % 128 // 16]] = m2
    dd = d0 - f1
    aa = a + f2
    y = pick8(dd, idx5, 16) + pick8(aa, idx6, 16)
    return y

@@ -1,0 +1,187 @@
+import concourse.mybir as mybir
+
+F32 = mybir.dt.float32
+BF16 = mybir.dt.bfloat16
+I32 = mybir.dt.int32
+U32 = mybir.dt.uint32
+U16 = mybir.dt.uint16
+U8 = mybir.dt.uint8
+FP8X4 = mybir.dt.float8_e4m3fn_x4
+FP4X4 = mybir.dt.float4_e2m1fn_x4
+ALU = mybir.AluOpType
+COPY = mybir.ActivationFunctionType.Copy
+
+P = 128
+PACK = 4
+Q = 128
+K = 512
+COLS = 1024
+BANK = 512
+SLOTS = 512
+HALF = SLOTS // 2
+FLOPS = 2 * 512 * 128 * (512 + 4 * 1024)
+SCALAR_ROWS = 32
+
+
+def tile_attend_innertwo_madefour_kernel(
+    tc, states, wq_words, wq_scales, keys_words, keys_scales, notes_words, notes_scales,
+    users_words, users_scales, shelves_words, shelves_scales,
+    offs, offs2, offs3, offs4, offs5, offs6, out,
+):
+    nc = tc.nc
+    with (
+        tc.tile_pool(name="held", bufs=1) as held,
+        tc.psum_pool(name="psum", bufs=1) as psum,
+    ):
+        def load_words8(name, words):
+            tile = held.tile([P, words.shape[2]], U32, name=name, align_bytes=64)
+            nc.sync.dma_start(tile[:].bitcast(I32), words[0].rearrange("p n t -> p (n t)").bitcast(I32))
+            return tile
+
+        def load_words4(name, words):
+            tile = held.tile([P, words.shape[2]], U8, name=name, align_bytes=64)
+            nc.sync.dma_start(tile[:].bitcast(I32), words[0].bitcast(I32))
+            return tile
+
+        def load_list(name, source):
+            tile = held.tile([P, SLOTS // 16], U16, name=name)
+            nc.sync.dma_start(tile[:], source)
+            return tile
+
+        def half_of(lst, h):
+            return lst[:, h * HALF // 16:(h + 1) * HALF // 16]
+
+        def cols(h):
+            return slice(h * HALF, (h + 1) * HALF)
+
+        widths = [K, COLS, COLS, COLS, COLS]
+        starts = [sum(widths[:j]) for j in range(5)]
+        planes = held.tile([P, sum(widths)], U8, name="planes", align_bytes=64)
+        nc.vector.memset(planes[:].bitcast(I32), 0)
+        staged = held.tile([16, sum(widths) // 4], I32, name="staged", align_bytes=64)
+        for j, scales in enumerate([wq_scales, users_scales, shelves_scales, keys_scales, notes_scales]):
+            nc.sync.dma_start(staged[:, starts[j] // 4:(starts[j] + widths[j]) // 4], scales[0].bitcast(I32))
+        states_raw = held.tile([P, PACK, Q], F32, name="states_raw")
+        nc.sync.dma_start(states_raw[:], states.rearrange("(p j) q -> p j q", j=PACK))
+        wq_raw = load_words8("wq_raw", wq_words)
+        users = load_words8("users", users_words)
+        for r in range(4):
+            nc.sync.dma_start(planes[:].bitcast(I32)[r:P:32, :], staged[r:16:4, :])
+        shelves = load_words4("shelves", shelves_words)
+        keys = load_words8("keys", keys_words)
+        notes = load_words4("notes", notes_words)
+        user_list = load_list("user_list", offs3)
+        shelf_list = load_list("shelf_list", offs4)
+        token_list = load_list("token_list", offs)
+        note_list = load_list("note_list", offs2)
+        shelf_pick = load_list("shelf_pick", offs5)
+        token_pick = load_list("token_pick", offs6)
+        wq_plane, users_plane, shelves_plane, keys_plane, notes_plane = [planes[:, starts[j]:starts[j] + widths[j]] for j in range(5)]
+
+        f1 = held.tile([P, COLS], F32, name="f1")
+        f2 = held.tile([P, COLS], F32, name="f2")
+        nc.vector.memset(f1[:], 0.0)
+        nc.vector.memset(f2[:], 0.0)
+
+        states_bf = held.tile([P, Q, PACK], BF16, name="states_bf", align_bytes=64)
+        def weave(lo, hi):
+            dst = states_bf[:, lo:hi, :].rearrange("p (c i) t -> p c t i", i=4)
+            src = states_raw[:, :, lo:hi].rearrange("p t (c i) -> p c t i", i=4)
+            return dst, src
+        nc.scalar.activation(*weave(0, SCALAR_ROWS), COPY)
+        nc.vector.tensor_copy(*weave(SCALAR_ROWS, Q))
+
+        wq_dealt = held.tile([P, K], U32, name="wq_dealt", align_bytes=64)
+        nc.scalar.copy(wq_dealt[:].rearrange("p (t m) -> p m t", t=PACK), wq_raw[:].rearrange("p (m t) -> p m t", t=PACK))
+        wq_plane_dealt = held.tile([P, K], U8, name="wq_plane_dealt", align_bytes=64)
+        nc.vector.tensor_copy(wq_plane_dealt[:].rearrange("p (t m) -> p m t", t=PACK), wq_plane.rearrange("p (m t) -> p m t", t=PACK))
+
+        def quantise(name, grouped):
+            codes = held.tile([P, Q], U32, name=name + "_codes", align_bytes=64)
+            plane = held.tile([P, Q], U8, name=name + "_plane", align_bytes=64)
+            nc.vector.quantize_mx(out=codes[:].bitcast(FP8X4), scales=plane[:], in_=grouped[:].rearrange("p q t -> p (q t)"))
+            return codes, plane
+
+        states_codes, states_plane = quantise("states", states_bf)
+
+        qv_bank = psum.tile([P, PACK, Q], F32, name="qv_bank", tag="shared_bank")
+        for t in range(PACK):
+            dealt = slice(t * P, (t + 1) * P)
+            nc.tensor.matmul_mx(
+                out=qv_bank[:, t, :], lhsT=wq_dealt[:, dealt].bitcast(FP8X4), lhsT_scale=wq_plane_dealt[:, dealt],
+                rhs=states_codes[:].bitcast(FP8X4), rhs_scale=states_plane[:], start=True, stop=True)
+        qv_bf = held.tile([P, Q, PACK], BF16, name="qv_bf", align_bytes=64)
+        nc.scalar.copy(qv_bf[:], qv_bank[:].rearrange("p t q -> p q t"))
+
+        qv_codes, qv_plane = quantise("qv", qv_bf)
+
+        def scores(name, codes, plane, words, table_plane, fp4, last_tag, first_copy):
+            tile = held.tile([P, COLS], F32, name=name)
+            banks = []
+            for h in range(2):
+                c = slice(h * BANK, (h + 1) * BANK)
+                bank = psum.tile([P, BANK], F32, name=name + "_bank%d" % h, tag=last_tag if h == 1 and last_tag else name + "_bank%d" % h)
+                moving = words[:, 2 * h * BANK:2 * (h + 1) * BANK].bitcast(FP4X4) if fp4 else words[:, c].bitcast(FP8X4)
+                nc.tensor.matmul_mx(out=bank[:], lhsT=codes[:].bitcast(FP8X4), lhsT_scale=plane[:],
+                                    rhs=moving, rhs_scale=table_plane[:, c], start=True, stop=True)
+                (first_copy if h == 0 else nc.scalar.copy)(tile[:, c], bank[:])
+                banks.append(bank)
+            return tile, banks
+
+        def slot_tile(name):
+            return held.tile([P, SLOTS], F32, name=name)
+
+        def gather_v(dst, table, lst, h):
+            nc.vector.tensor_copy(dst, table[:].indirect(half_of(lst, h)))
+
+        def gather_s(dst, table, lst, h):
+            nc.scalar.activation(dst, table[:].indirect(half_of(lst, h)), COPY)
+
+        first = held.tile([P, 4, HALF], F32, name="first")
+        c0, c_banks = scores("c0", states_codes, states_plane, users, users_plane, False, None, nc.vector.tensor_copy)
+        gather_v(first[:, 1, :], c0, user_list, 0)
+        d0, d_banks = scores("d0", states_codes, states_plane, shelves, shelves_plane, True, None, nc.scalar.copy)
+        a, a_banks = scores("a", qv_codes, qv_plane, keys, keys_plane, False, None, nc.vector.tensor_copy)
+        gather_v(first[:, 3, :], d0, shelf_list, 0)
+        b, b_banks = scores("b", qv_codes, qv_plane, notes, notes_plane, True, "shared_bank", nc.vector.tensor_copy)
+        gather_s(first[:, 0, :], a, token_list, 0)
+        gather_v(first[:, 2, :], b, note_list, 0)
+        second = held.tile([P, 4, HALF], F32, name="second", tag="notes", align_bytes=64)
+        gather_s(second[:, 1, :], c0, user_list, 1)
+        gather_s(second[:, 3, :], d0, shelf_list, 1)
+        gather_s(second[:, 0, :], a, token_list, 1)
+        gather_s(second[:, 2, :], b, note_list, 1)
+
+        m1 = slot_tile("m1")
+        m2 = slot_tile("m2")
+        hi = held.tile([P, 2, 2, HALF], F32, name="hi")
+        lo = held.tile([P, 2, 2, HALF], F32, name="lo")
+        for j in (1, 0):
+            nc.vector.tensor_tensor(hi[:, 0, j, :], first[:, j, :], first[:, 2 + j, :], ALU.max)
+            nc.vector.tensor_tensor(lo[:, 0, j, :], first[:, j, :], first[:, 2 + j, :], ALU.min)
+        for h in range(2):
+            s = cols(h)
+            if h == 1:
+                nc.vector.tensor_tensor(hi[:, 1, :, :], second[:, 0:2, :], second[:, 2:4, :], ALU.max)
+                nc.vector.tensor_tensor(lo[:, 1, :, :], second[:, 0:2, :], second[:, 2:4, :], ALU.min)
+            nc.vector.tensor_tensor(m1[:, s], hi[:, h, 0, :], hi[:, h, 1, :], ALU.min)
+            nc.vector.tensor_tensor(m2[:, s], lo[:, h, 0, :], lo[:, h, 1, :], ALU.max)
+            nc.vector.tensor_copy(f1[:].indirect(half_of(shelf_list, h)), m1[:, s])
+        nc.vector.tensor_copy(f2[:].indirect(token_list[:]), m2[:])
+
+        dd = held.tile([P, COLS], F32, name="dd")
+        nc.gpsimd.tensor_tensor(dd[:], d0[:], f1[:], ALU.subtract)
+        ddg = slot_tile("ddg")
+        nc.scalar.activation(ddg[:], dd[:].indirect(shelf_pick[:]), COPY)
+
+        aa = held.tile([P, COLS], F32, name="aa")
+        for h in range(2):
+            c = slice(h * BANK, (h + 1) * BANK)
+            nc.vector.tensor_tensor(aa[:, c], a_banks[h][:], f2[:, c], ALU.add)
+        result = slot_tile("result")
+        aag = held.tile([P, HALF], F32, name="aag")
+        nc.scalar.activation(aag[:], aa[:].indirect(half_of(token_pick, 1)), COPY)
+        nc.vector.tensor_tensor(result[:, cols(0)], aa[:].indirect(half_of(token_pick, 0)), ddg[:, cols(0)], ALU.add)
+        nc.sync.dma_start(out[:, cols(0)], result[:, cols(0)])
+        nc.vector.tensor_tensor(result[:, cols(1)], aag[:], ddg[:, cols(1)], ALU.add)
+        nc.sync.dma_start(out[:, cols(1)], result[:, cols(1)])

@@ -21,6 +21,7 @@ SLOTS = 512
 HALF = SLOTS // 2
 FLOPS = 2 * 512 * 128 * (512 + 4 * 1024)
 SCALAR_ROWS = 32
+EARLY = 128
 
 
 def tile_attend_innertwo_madefour_kernel(
@@ -54,29 +55,38 @@ def tile_attend_innertwo_madefour_kernel(
         def cols(h):
             return slice(h * HALF, (h + 1) * HALF)
 
-        widths = [K, COLS, COLS, COLS, COLS]
-        starts = [sum(widths[:j]) for j in range(5)]
-        planes = held.tile([P, sum(widths)], U8, name="planes", align_bytes=64)
-        nc.vector.memset(planes[:].bitcast(I32), 0)
-        staged = held.tile([16, sum(widths) // 4], I32, name="staged", align_bytes=64)
-        for j, scales in enumerate([wq_scales, users_scales, shelves_scales, keys_scales, notes_scales]):
-            nc.sync.dma_start(staged[:, starts[j] // 4:(starts[j] + widths[j]) // 4], scales[0].bitcast(I32))
+        def staged_scales(name, tables):
+            widths = [scales.shape[2] for scales in tables]
+            starts = [sum(widths[:j]) for j in range(len(tables))]
+            planes = held.tile([P, sum(widths)], U8, name=name + "_planes", align_bytes=64)
+            nc.vector.memset(planes[:].bitcast(I32), 0)
+            staged = held.tile([16, sum(widths) // 4], I32, name=name + "_staged", align_bytes=64)
+            for start, width, scales in zip(starts, widths, tables):
+                nc.sync.dma_start(staged[:, start // 4:(start + width) // 4], scales[0].bitcast(I32))
+            return planes, staged, [planes[:, start:start + width] for start, width in zip(starts, widths)]
+
+        def spread(planes, staged, queue):
+            for r in range(4):
+                queue.dma_start(planes[:].bitcast(I32)[r:P:32, :], staged[r:16:4, :])
+
+        early_planes, early_staged, (wq_plane, users_plane, shelves_plane) = staged_scales(
+            "early", [wq_scales, users_scales, shelves_scales])
+        late_planes, late_staged, (keys_plane, notes_plane) = staged_scales("late", [keys_scales, notes_scales])
         states_raw = held.tile([P, PACK, Q], F32, name="states_raw")
         nc.sync.dma_start(states_raw[:], states.rearrange("(p j) q -> p j q", j=PACK))
         wq_raw = load_words8("wq_raw", wq_words)
+        spread(early_planes, early_staged, nc.scalar)
         users = load_words8("users", users_words)
-        for r in range(4):
-            nc.sync.dma_start(planes[:].bitcast(I32)[r:P:32, :], staged[r:16:4, :])
         shelves = load_words4("shelves", shelves_words)
-        keys = load_words8("keys", keys_words)
-        notes = load_words4("notes", notes_words)
         user_list = load_list("user_list", offs3)
         shelf_list = load_list("shelf_list", offs4)
+        keys = load_words8("keys", keys_words)
+        spread(late_planes, late_staged, nc.sync)
+        notes = load_words4("notes", notes_words)
         token_list = load_list("token_list", offs)
         note_list = load_list("note_list", offs2)
         shelf_pick = load_list("shelf_pick", offs5)
         token_pick = load_list("token_pick", offs6)
-        wq_plane, users_plane, shelves_plane, keys_plane, notes_plane = [planes[:, starts[j]:starts[j] + widths[j]] for j in range(5)]
 
         f1 = held.tile([P, COLS], F32, name="f1")
         f2 = held.tile([P, COLS], F32, name="f2")
@@ -88,11 +98,10 @@ def tile_attend_innertwo_madefour_kernel(
             dst = states_bf[:, lo:hi, :].rearrange("p (c i) t -> p c t i", i=4)
             src = states_raw[:, :, lo:hi].rearrange("p t (c i) -> p c t i", i=4)
             return dst, src
-        nc.scalar.activation(*weave(0, SCALAR_ROWS), COPY)
-        nc.vector.tensor_copy(*weave(SCALAR_ROWS, Q))
+        nc.vector.tensor_copy(*weave(0, Q))
 
         wq_dealt = held.tile([P, K], U32, name="wq_dealt", align_bytes=64)
-        nc.scalar.copy(wq_dealt[:].rearrange("p (t m) -> p m t", t=PACK), wq_raw[:].rearrange("p (m t) -> p m t", t=PACK))
+        nc.vector.tensor_copy(wq_dealt[:].bitcast(I32).rearrange("p (t m) -> p m t", t=PACK), wq_raw[:].bitcast(I32).rearrange("p (m t) -> p m t", t=PACK))
         wq_plane_dealt = held.tile([P, K], U8, name="wq_plane_dealt", align_bytes=64)
         nc.vector.tensor_copy(wq_plane_dealt[:].rearrange("p (t m) -> p m t", t=PACK), wq_plane.rearrange("p (m t) -> p m t", t=PACK))
 
@@ -115,7 +124,7 @@ def tile_attend_innertwo_madefour_kernel(
 
         qv_codes, qv_plane = quantise("qv", qv_bf)
 
-        def scores(name, codes, plane, words, table_plane, fp4, last_tag, first_copy):
+        def scores(name, codes, plane, words, table_plane, fp4, last_tag, copies):
             tile = held.tile([P, COLS], F32, name=name)
             banks = []
             for h in range(2):
@@ -124,7 +133,7 @@ def tile_attend_innertwo_madefour_kernel(
                 moving = words[:, 2 * h * BANK:2 * (h + 1) * BANK].bitcast(FP4X4) if fp4 else words[:, c].bitcast(FP8X4)
                 nc.tensor.matmul_mx(out=bank[:], lhsT=codes[:].bitcast(FP8X4), lhsT_scale=plane[:],
                                     rhs=moving, rhs_scale=table_plane[:, c], start=True, stop=True)
-                (first_copy if h == 0 else nc.scalar.copy)(tile[:, c], bank[:])
+                copies[h](tile[:, c], bank[:])
                 banks.append(bank)
             return tile, banks
 
@@ -138,15 +147,19 @@ def tile_attend_innertwo_madefour_kernel(
             nc.scalar.activation(dst, table[:].indirect(half_of(lst, h)), COPY)
 
         first = held.tile([P, 4, HALF], F32, name="first")
-        c0, c_banks = scores("c0", states_codes, states_plane, users, users_plane, False, None, nc.vector.tensor_copy)
+        c0, c_banks = scores("c0", states_codes, states_plane, users, users_plane, False, None, [nc.vector.tensor_copy, lambda dst, src: nc.scalar.activation(dst, src, COPY)])
         gather_v(first[:, 1, :], c0, user_list, 0)
-        d0, d_banks = scores("d0", states_codes, states_plane, shelves, shelves_plane, True, None, nc.scalar.copy)
-        a, a_banks = scores("a", qv_codes, qv_plane, keys, keys_plane, False, None, nc.vector.tensor_copy)
+        d0, d_banks = scores("d0", states_codes, states_plane, shelves, shelves_plane, True, "shared_bank", [nc.scalar.copy, nc.vector.tensor_copy])
+        a, a_banks = scores("a", qv_codes, qv_plane, keys, keys_plane, False, None, [nc.scalar.copy] * 2)
         gather_v(first[:, 3, :], d0, shelf_list, 0)
-        b, b_banks = scores("b", qv_codes, qv_plane, notes, notes_plane, True, "shared_bank", nc.vector.tensor_copy)
-        gather_s(first[:, 0, :], a, token_list, 0)
+        hi = held.tile([P, 2, 2, HALF], F32, name="hi")
+        lo = held.tile([P, 2, 2, HALF], F32, name="lo")
+        nc.vector.tensor_tensor(hi[:, 0, 1, :], first[:, 1, :], first[:, 3, :], ALU.max)
+        nc.vector.tensor_tensor(lo[:, 0, 1, :], first[:, 1, :], first[:, 3, :], ALU.min)
+        b, b_banks = scores("b", qv_codes, qv_plane, notes, notes_plane, True, None, [nc.vector.tensor_copy, nc.scalar.copy])
+        second = held.tile([P, 5, HALF], F32, name="second", tag="notes", align_bytes=64)
+        gather_s(second[:, 4, :], a, token_list, 0)
         gather_v(first[:, 2, :], b, note_list, 0)
-        second = held.tile([P, 4, HALF], F32, name="second", tag="notes", align_bytes=64)
         gather_s(second[:, 1, :], c0, user_list, 1)
         gather_s(second[:, 3, :], d0, shelf_list, 1)
         gather_s(second[:, 0, :], a, token_list, 1)
@@ -154,11 +167,8 @@ def tile_attend_innertwo_madefour_kernel(
 
         m1 = slot_tile("m1")
         m2 = slot_tile("m2")
-        hi = held.tile([P, 2, 2, HALF], F32, name="hi")
-        lo = held.tile([P, 2, 2, HALF], F32, name="lo")
-        for j in (1, 0):
-            nc.vector.tensor_tensor(hi[:, 0, j, :], first[:, j, :], first[:, 2 + j, :], ALU.max)
-            nc.vector.tensor_tensor(lo[:, 0, j, :], first[:, j, :], first[:, 2 + j, :], ALU.min)
+        nc.vector.tensor_tensor(hi[:, 0, 0, :], second[:, 4, :], first[:, 2, :], ALU.max)
+        nc.vector.tensor_tensor(lo[:, 0, 0, :], second[:, 4, :], first[:, 2, :], ALU.min)
         for h in range(2):
             s = cols(h)
             if h == 1:
@@ -172,7 +182,8 @@ def tile_attend_innertwo_madefour_kernel(
         dd = held.tile([P, COLS], F32, name="dd")
         nc.gpsimd.tensor_tensor(dd[:], d0[:], f1[:], ALU.subtract)
         ddg = slot_tile("ddg")
-        nc.scalar.activation(ddg[:], dd[:].indirect(shelf_pick[:]), COPY)
+        for h in range(2):
+            gather_s(ddg[:, cols(h)], dd, shelf_pick, h)
 
         aa = held.tile([P, COLS], F32, name="aa")
         for h in range(2):

import concourse.mybir as mybir

F32 = mybir.dt.float32
BF16 = mybir.dt.bfloat16
I32 = mybir.dt.int32
U32 = mybir.dt.uint32
U16 = mybir.dt.uint16
U8 = mybir.dt.uint8
FP8X4 = mybir.dt.float8_e4m3fn_x4
FP4X4 = mybir.dt.float4_e2m1fn_x4
ALU = mybir.AluOpType
COPY = mybir.ActivationFunctionType.Copy

P = 128
PACK = 4
Q = 128
K = 512
COLS = 1024
BANK = 512
SLOTS = 512
HALF = SLOTS // 2
FLOPS = 2 * 512 * 128 * (512 + 4 * 1024)
SCALAR_ROWS = 32
EARLY = 128


def tile_attend_innertwo_madefour_kernel(
    tc, states, wq_words, wq_scales, keys_words, keys_scales, notes_words, notes_scales,
    users_words, users_scales, shelves_words, shelves_scales,
    offs, offs2, offs3, offs4, offs5, offs6, out,
):
    nc = tc.nc
    with (
        tc.tile_pool(name="held", bufs=1) as held,
        tc.psum_pool(name="psum", bufs=1) as psum,
    ):
        def load_words8(name, words):
            tile = held.tile([P, words.shape[2]], U32, name=name, align_bytes=64)
            nc.sync.dma_start(tile[:].bitcast(I32), words[0].rearrange("p n t -> p (n t)").bitcast(I32))
            return tile

        def load_words4(name, words):
            tile = held.tile([P, words.shape[2]], U8, name=name, align_bytes=64)
            nc.sync.dma_start(tile[:].bitcast(I32), words[0].bitcast(I32))
            return tile

        def load_list(name, source):
            tile = held.tile([P, SLOTS // 16], U16, name=name)
            nc.sync.dma_start(tile[:], source)
            return tile

        def half_of(lst, h):
            return lst[:, h * HALF // 16:(h + 1) * HALF // 16]

        def cols(h):
            return slice(h * HALF, (h + 1) * HALF)

        def staged_scales(name, tables):
            widths = [scales.shape[2] for scales in tables]
            starts = [sum(widths[:j]) for j in range(len(tables))]
            planes = held.tile([P, sum(widths)], U8, name=name + "_planes", align_bytes=64)
            nc.vector.memset(planes[:].bitcast(I32), 0)
            staged = held.tile([16, sum(widths) // 4], I32, name=name + "_staged", align_bytes=64)
            for start, width, scales in zip(starts, widths, tables):
                nc.sync.dma_start(staged[:, start // 4:(start + width) // 4], scales[0].bitcast(I32))
            return planes, staged, [planes[:, start:start + width] for start, width in zip(starts, widths)]

        def spread(planes, staged, queue):
            for r in range(4):
                queue.dma_start(planes[:].bitcast(I32)[r:P:32, :], staged[r:16:4, :])

        early_planes, early_staged, (wq_plane, users_plane, shelves_plane) = staged_scales(
            "early", [wq_scales, users_scales, shelves_scales])
        late_planes, late_staged, (keys_plane, notes_plane) = staged_scales("late", [keys_scales, notes_scales])
        states_raw = held.tile([P, PACK, Q], F32, name="states_raw")
        nc.sync.dma_start(states_raw[:], states.rearrange("(p j) q -> p j q", j=PACK))
        wq_raw = load_words8("wq_raw", wq_words)
        spread(early_planes, early_staged, nc.scalar)
        users = load_words8("users", users_words)
        shelves = load_words4("shelves", shelves_words)
        user_list = load_list("user_list", offs3)
        shelf_list = load_list("shelf_list", offs4)
        keys = load_words8("keys", keys_words)
        spread(late_planes, late_staged, nc.sync)
        notes = load_words4("notes", notes_words)
        token_list = load_list("token_list", offs)
        note_list = load_list("note_list", offs2)
        shelf_pick = load_list("shelf_pick", offs5)
        token_pick = load_list("token_pick", offs6)

        f1 = held.tile([P, COLS], F32, name="f1")
        f2 = held.tile([P, COLS], F32, name="f2")
        nc.vector.memset(f1[:], 0.0)
        nc.vector.memset(f2[:], 0.0)

        states_bf = held.tile([P, Q, PACK], BF16, name="states_bf", align_bytes=64)
        def weave(lo, hi):
            dst = states_bf[:, lo:hi, :].rearrange("p (c i) t -> p c t i", i=4)
            src = states_raw[:, :, lo:hi].rearrange("p t (c i) -> p c t i", i=4)
            return dst, src
        nc.vector.tensor_copy(*weave(0, Q))

        wq_dealt = held.tile([P, K], U32, name="wq_dealt", align_bytes=64)
        nc.vector.tensor_copy(wq_dealt[:].bitcast(I32).rearrange("p (t m) -> p m t", t=PACK), wq_raw[:].bitcast(I32).rearrange("p (m t) -> p m t", t=PACK))
        wq_plane_dealt = held.tile([P, K], U8, name="wq_plane_dealt", align_bytes=64)
        nc.vector.tensor_copy(wq_plane_dealt[:].rearrange("p (t m) -> p m t", t=PACK), wq_plane.rearrange("p (m t) -> p m t", t=PACK))

        def quantise(name, grouped):
            codes = held.tile([P, Q], U32, name=name + "_codes", align_bytes=64)
            plane = held.tile([P, Q], U8, name=name + "_plane", align_bytes=64)
            nc.vector.quantize_mx(out=codes[:].bitcast(FP8X4), scales=plane[:], in_=grouped[:].rearrange("p q t -> p (q t)"))
            return codes, plane

        states_codes, states_plane = quantise("states", states_bf)

        qv_bank = psum.tile([P, PACK, Q], F32, name="qv_bank", tag="shared_bank")
        for t in range(PACK):
            dealt = slice(t * P, (t + 1) * P)
            nc.tensor.matmul_mx(
                out=qv_bank[:, t, :], lhsT=wq_dealt[:, dealt].bitcast(FP8X4), lhsT_scale=wq_plane_dealt[:, dealt],
                rhs=states_codes[:].bitcast(FP8X4), rhs_scale=states_plane[:], start=True, stop=True)
        qv_bf = held.tile([P, Q, PACK], BF16, name="qv_bf", align_bytes=64)
        nc.scalar.copy(qv_bf[:], qv_bank[:].rearrange("p t q -> p q t"))

        qv_codes, qv_plane = quantise("qv", qv_bf)

        def scores(name, codes, plane, words, table_plane, fp4, last_tag, copies):
            tile = held.tile([P, COLS], F32, name=name)
            banks = []
            for h in range(2):
                c = slice(h * BANK, (h + 1) * BANK)
                bank = psum.tile([P, BANK], F32, name=name + "_bank%d" % h, tag=last_tag if h == 1 and last_tag else name + "_bank%d" % h)
                moving = words[:, 2 * h * BANK:2 * (h + 1) * BANK].bitcast(FP4X4) if fp4 else words[:, c].bitcast(FP8X4)
                nc.tensor.matmul_mx(out=bank[:], lhsT=codes[:].bitcast(FP8X4), lhsT_scale=plane[:],
                                    rhs=moving, rhs_scale=table_plane[:, c], start=True, stop=True)
                copies[h](tile[:, c], bank[:])
                banks.append(bank)
            return tile, banks

        def slot_tile(name):
            return held.tile([P, SLOTS], F32, name=name)

        def gather_v(dst, table, lst, h):
            nc.vector.tensor_copy(dst, table[:].indirect(half_of(lst, h)))

        def gather_s(dst, table, lst, h):
            nc.scalar.activation(dst, table[:].indirect(half_of(lst, h)), COPY)

        first = held.tile([P, 4, HALF], F32, name="first")
        c0, c_banks = scores("c0", states_codes, states_plane, users, users_plane, False, None, [nc.vector.tensor_copy, lambda dst, src: nc.scalar.activation(dst, src, COPY)])
        gather_v(first[:, 1, :], c0, user_list, 0)
        d0, d_banks = scores("d0", states_codes, states_plane, shelves, shelves_plane, True, "shared_bank", [nc.scalar.copy, nc.vector.tensor_copy])
        a, a_banks = scores("a", qv_codes, qv_plane, keys, keys_plane, False, None, [nc.scalar.copy] * 2)
        gather_v(first[:, 3, :], d0, shelf_list, 0)
        hi = held.tile([P, 2, 2, HALF], F32, name="hi")
        lo = held.tile([P, 2, 2, HALF], F32, name="lo")
        nc.vector.tensor_tensor(hi[:, 0, 1, :], first[:, 1, :], first[:, 3, :], ALU.max)
        nc.vector.tensor_tensor(lo[:, 0, 1, :], first[:, 1, :], first[:, 3, :], ALU.min)
        b, b_banks = scores("b", qv_codes, qv_plane, notes, notes_plane, True, None, [nc.vector.tensor_copy, nc.scalar.copy])
        second = held.tile([P, 5, HALF], F32, name="second", tag="notes", align_bytes=64)
        gather_s(second[:, 4, :], a, token_list, 0)
        gather_v(first[:, 2, :], b, note_list, 0)
        gather_s(second[:, 1, :], c0, user_list, 1)
        gather_s(second[:, 3, :], d0, shelf_list, 1)
        gather_s(second[:, 0, :], a, token_list, 1)
        gather_s(second[:, 2, :], b, note_list, 1)

        m1 = slot_tile("m1")
        m2 = slot_tile("m2")
        nc.vector.tensor_tensor(hi[:, 0, 0, :], second[:, 4, :], first[:, 2, :], ALU.max)
        nc.vector.tensor_tensor(lo[:, 0, 0, :], second[:, 4, :], first[:, 2, :], ALU.min)
        for h in range(2):
            s = cols(h)
            if h == 1:
                nc.vector.tensor_tensor(hi[:, 1, :, :], second[:, 0:2, :], second[:, 2:4, :], ALU.max)
                nc.vector.tensor_tensor(lo[:, 1, :, :], second[:, 0:2, :], second[:, 2:4, :], ALU.min)
            nc.vector.tensor_tensor(m1[:, s], hi[:, h, 0, :], hi[:, h, 1, :], ALU.min)
            nc.vector.tensor_tensor(m2[:, s], lo[:, h, 0, :], lo[:, h, 1, :], ALU.max)
            nc.vector.tensor_copy(f1[:].indirect(half_of(shelf_list, h)), m1[:, s])
        nc.vector.tensor_copy(f2[:].indirect(token_list[:]), m2[:])

        dd = held.tile([P, COLS], F32, name="dd")
        nc.gpsimd.tensor_tensor(dd[:], d0[:], f1[:], ALU.subtract)
        ddg = slot_tile("ddg")
        for h in range(2):
            gather_s(ddg[:, cols(h)], dd, shelf_pick, h)

        aa = held.tile([P, COLS], F32, name="aa")
        for h in range(2):
            c = slice(h * BANK, (h + 1) * BANK)
            nc.vector.tensor_tensor(aa[:, c], a_banks[h][:], f2[:, c], ALU.add)
        result = slot_tile("result")
        aag = held.tile([P, HALF], F32, name="aag")
        nc.scalar.activation(aag[:], aa[:].indirect(half_of(token_pick, 1)), COPY)
        nc.vector.tensor_tensor(result[:, cols(0)], aa[:].indirect(half_of(token_pick, 0)), ddg[:, cols(0)], ALU.add)
        nc.sync.dma_start(out[:, cols(0)], result[:, cols(0)])
        nc.vector.tensor_tensor(result[:, cols(1)], aag[:], ddg[:, cols(1)], ALU.add)
        nc.sync.dma_start(out[:, cols(1)], result[:, cols(1)])
